import numpy as np
import ml_dtypes


def mxq(x, axis, fmt="e4m3"):
    dtype, down = {"e4m3": (ml_dtypes.float8_e4m3fn, 7), "e5m2": (ml_dtypes.float8_e5m2, 14)}[fmt]
    v = np.moveaxis(np.asarray(x, np.float32).astype(ml_dtypes.bfloat16).astype(np.float64), axis, -1)
    blocks = v.reshape(v.shape[:-1] + (-1, 32))
    amax = np.abs(blocks).max(-1, keepdims=True)
    byte = np.maximum(np.where(amax > 0, np.frexp(amax)[1] - 1 + 127, 0) - down, 1)
    scale = np.exp2(byte - 127.0)
    codes = (blocks / scale).astype(np.float32).astype(dtype).astype(np.float64)
    return np.moveaxis((codes * scale).reshape(v.shape), -1, axis)


WIDE = False


def mx_kscale(k):
    if not WIDE:
        return np.ones(k)
    levels = np.array([10, -10, 5, -5, 0])
    if k % 512:
        return np.exp2(np.random.permutation(np.resize(levels, k // 32))).repeat(32)
    a = np.empty((k // 512, 16))
    for p in range(k // 512):
        a[p, :8] = np.random.permutation(np.resize(levels, 8))
        for g in range(8):
            far = levels[np.abs(levels - a[p, g]) >= 10]
            a[p, g + 8] = far[np.random.randint(len(far))]
    return np.exp2(a.ravel()).repeat(32)


def f64(x):
    return np.asarray(x).astype(np.float64)


def striped(idx):
    return np.tile(idx.reshape(-1, 16).T, (8, 1)).astype(np.uint16)


def unstriped(offs):
    return offs[:16].T.reshape(-1).astype(np.int64)


E2M1 = np.array([0.0, 0.5, 1.0, 1.5, 2.0, 3.0, 4.0, 6.0, -0.0, -0.5, -1.0, -1.5, -2.0, -3.0, -4.0, -6.0])


def pack_fp4(w):
    k, n = w.shape
    w = f64(np.asarray(w, np.float32).astype(ml_dtypes.bfloat16)).reshape(k // 32, 32, n)
    amax = np.abs(w).max(1)
    mant, ex = np.frexp(amax / 6.0)
    byte = np.clip(np.where(amax > 0, np.where(mant > 0.5, ex, ex - 1) + 127, 1), 1, 254)
    scaled = (w * np.exp2(127.0 - byte)[:, None, :]).reshape(k, n).astype(np.float32)
    c = np.ascontiguousarray(scaled.reshape(k // 512, 128, 4, n).transpose(0, 1, 3, 2)).astype(ml_dtypes.float4_e2m1fn).view(np.uint8) & 0xF
    words = (c[..., 0::2] | (c[..., 1::2] << 4)).reshape(k // 512, 128, 2 * n)
    return np.ascontiguousarray(words), np.ascontiguousarray(byte.astype(np.uint8).reshape(k // 512, 16, n))


def unpack_fp4(words, scales):
    g, _, n = scales.shape
    words = np.ascontiguousarray(words).reshape(g, 128, n, 2)
    nib = np.empty((g, 128, n, 4), np.uint8)
    nib[..., 0::2] = words & 0xF
    nib[..., 1::2] = words >> 4
    vals = E2M1[nib] * np.repeat(np.exp2(scales.astype(np.float64) - 127.0), 8, axis=1)[..., None]
    return vals.transpose(0, 1, 3, 2).reshape(g * 512, n)


K, T, S, V, N, U = 1024, 2048, 1536, 512, 128, 1024


def setup_inputs():
    n = np.random.standard_normal
    s = mx_kscale(K)[:, None]
    packed_w1 = pack_fp4(n((K, N)) / np.sqrt(3 * K) / s)
    packed_w2 = pack_fp4(n((K, N)) / np.sqrt(3 * K) / s)
    packed_w3 = pack_fp4(n((K, N)) / np.sqrt(3 * K) / s)
    return {
        "xT": (n((K, T)) * s).astype(np.float32),
        "w1_words": packed_w1[0],
        "w1_scales": packed_w1[1],
        "w2_words": packed_w2[0],
        "w2_scales": packed_w2[1],
        "w3_words": packed_w3[0],
        "w3_scales": packed_w3[1],
        "offs": striped(np.random.permutation(T)[:S]),
        "to1": striped(np.random.permutation(U)[:V]),
        "to2": striped(np.random.permutation(U)[:V]),
        "to3": striped(np.random.permutation(U)[:V]),
    }


def reference(xT, w1_words, w1_scales, w2_words, w2_scales, w3_words, w3_scales, offs, to1, to2, to3):
    xq = mxq(f64(xT)[:, unstriped(offs)], 0, "e4m3")
    o0 = np.zeros((N, U))
    o0[:, unstriped(to1)] = unpack_fp4(w1_words, w1_scales).T @ xq[:, :V]
    o1 = np.zeros((N, U))
    o1[:, unstriped(to2)] = unpack_fp4(w2_words, w2_scales).T @ xq[:, V:2 * V]
    o2 = np.zeros((N, U))
    o2[:, unstriped(to3)] = unpack_fp4(w3_words, w3_scales).T @ xq[:, 2 * V:3 * V]
    return o0 + o1 + o2

@@ -1,0 +1,174 @@
+from contextlib import ExitStack
+
+import concourse.mybir as mybir
+from concourse.masks import make_identity
+
+K, T, V, N, U = 1024, 2048, 512, 128, 1024
+TAPS = 3
+FLOPS = 2 * K * N * TAPS * V
+
+F32 = mybir.dt.float32
+BF16 = mybir.dt.bfloat16
+I32 = mybir.dt.int32
+U32 = mybir.dt.uint32
+U16 = mybir.dt.uint16
+U8 = mybir.dt.uint8
+FP8X4 = mybir.dt.float8_e4m3fn_x4
+FP4X4 = mybir.dt.float4_e2m1fn_x4
+ADD = mybir.AluOpType.add
+
+P = 128
+PASSES = 2
+BANK = 512
+LIST_COLS = V // 16
+
+CHUNKS = (
+    ((1024, 0), (1024, 640)),
+    ((512, 0), (512, 0), (512, 0), (512, 320)),
+    ((512, 0), (512, 0), (512, 0), (512, 0)),
+    ((512, 0), (512, 0), (512, 0), (512, 256)),
+)
+
+
+def tile_picked_spconv_none_e_kernel(tc, xT, w1_words, w1_scales, w2_words, w2_scales, w3_words, w3_scales, offs, to1, to2, to3, out):
+    nc = tc.nc
+    w_words = (w1_words, w2_words, w3_words)
+    w_scales = (w1_scales, w2_scales, w3_scales)
+    to_lists = (to1, to2, to3)
+    x_rows = xT.rearrange("(g p u e) t -> g u p e t", g=PASSES, p=P, u=2, e=2)
+
+    with ExitStack() as ctx:
+        keep = ctx.enter_context(tc.tile_pool(name="keep", bufs=1))
+        psum = ctx.enter_context(tc.psum_pool(name="psum", bufs=1))
+
+        offs_sb = keep.tile([P, TAPS * LIST_COLS], U16, name="offs_sb")
+        to_sb = [keep.tile([P, LIST_COLS], U16, name=f"to{d}") for d in range(TAPS)]
+        wq = [keep.tile([P, PASSES, 2 * N], U8, name=f"wq{d}", align_bytes=64) for d in range(TAPS)]
+        ws = [keep.tile([P, PASSES, N], U8, name=f"ws{d}", align_bytes=64) for d in range(TAPS)]
+        for d in range(TAPS):
+            nc.vector.memset(ws[d][:].bitcast(I32), 0)
+        for d in range(TAPS):
+            for q in range(4):
+                nc.gpsimd.dma_start(
+                    out=ws[d][32 * q : 32 * q + 4, :, :].bitcast(I32),
+                    in_=w_scales[d][:, 4 * q : 4 * q + 4, :].rearrange("g r c -> r g c").bitcast(I32),
+                )
+        ident = keep.tile([P, P], F32, name="ident")
+        make_identity(nc, ident[:])
+        placed = [keep.tile([P, U], F32, name=f"placed{d}") for d in range(TAPS)]
+        for d in range(TAPS):
+            nc.vector.memset(placed[d][:], 0.0)
+
+        small = [lambda: nc.sync.dma_start(offs_sb[:], offs)]
+        for d in range(TAPS):
+            small.append(lambda d=d: nc.sync.dma_start(
+                out=wq[d][:].bitcast(I32), in_=w_words[d].rearrange("g p c -> p g c").bitcast(I32)))
+        for d in range(TAPS):
+            small.append(lambda d=d: nc.sync.dma_start(to_sb[d][:], to_lists[d]))
+
+        raw = {}
+        for i in range(4):
+            c0 = 0
+            for j, (width, vshare) in enumerate(CHUNKS[i]):
+                raw[i, j] = keep.tile([P, 2, width], F32, name=f"raw{i}_{j}", tag=f"raw{i}_{j}", align_bytes=64)
+                nc.sync.dma_start(out=raw[i, j][:], in_=x_rows[i // 2, i % 2][:, :, c0 : c0 + width])
+                if small and ((i, j) == (0, 0) or i >= 2):
+                    small.pop(0)()
+                c0 = c0 + width
+
+        pairs = [keep.tile([P, T, 2], BF16, name=f"pairs{i}", align_bytes=64) for i in range(4)]
+        picked = {(g, d): keep.tile([P, 2, V], U32, name=f"picked{g}_{d}") for g in range(PASSES) for d in range(TAPS)}
+        acc = [psum.tile([P, V], F32, name=f"acc{d}") for d in range(TAPS)]
+        quads = {}
+
+        def cast(i):
+            c0 = 0
+            for j, (width, vshare) in enumerate(CHUNKS[i]):
+                s = width - vshare
+                src = raw[i, j][:].rearrange("p e t -> p t e")
+                if vshare:
+                    nc.vector.tensor_copy(out=pairs[i][:, c0 + s : c0 + width, :], in_=src[:, s:width, :])
+                if s:
+                    nc.scalar.copy(out=pairs[i][:, c0 : c0 + s, :], in_=src[:, 0:s, :])
+                c0 = c0 + width
+
+        def gather(i, d):
+            window = pairs[i][:].rearrange("p t e -> p (t e)").bitcast(U32)
+            nc.vector.tensor_copy(
+                out=picked[i // 2, d][:, i % 2, :],
+                in_=window.indirect(offs_sb[:, d * LIST_COLS : (d + 1) * LIST_COLS]),
+            )
+
+        def weave(g, d, on_vector):
+            tag = "raw3_3" if (g, d) == (0, TAPS - 1) else f"quads{g}_{d}"
+            quads[g, d] = keep.tile([P, 4 * V], BF16, name=f"quads{g}_{d}", tag=tag, align_bytes=64)
+            if on_vector:
+                nc.vector.tensor_copy(
+                    out=quads[g, d][:].bitcast(I32).rearrange("p (v u) -> p v u", u=2),
+                    in_=picked[g, d][:].bitcast(I32).rearrange("p u v -> p v u"))
+            else:
+                nc.scalar.copy(
+                    out=quads[g, d][:].bitcast(U32).rearrange("p (v u) -> p v u", u=2),
+                    in_=picked[g, d][:].rearrange("p u v -> p v u"))
+
+        def multiply(g, d):
+            codes = keep.tile([P, V], U32, name=f"codes{g}_{d}", align_bytes=64)
+            scales = keep.tile([P, V], U8, name=f"scales{g}_{d}", align_bytes=64)
+            nc.vector.quantize_mx(out=codes[:].bitcast(FP8X4), scales=scales[:], in_=quads[g, d][:])
+            nc.tensor.matmul_mx(
+                out=acc[d][:], lhsT=wq[d][:, g, :].bitcast(FP4X4), lhsT_scale=ws[d][:, g, :],
+                rhs=codes[:].bitcast(FP8X4), rhs_scale=scales[:], start=(g == 0), stop=(g == PASSES - 1))
+
+        def place(d):
+            y = keep.tile([P, V], F32, name=f"y{d}")
+            nc.scalar.copy(out=y[:], in_=acc[d][:])
+            nc.vector.tensor_copy(out=placed[d][:].indirect(to_sb[d][:]), in_=y[:])
+
+        cast(0)
+        for d in range(TAPS):
+            gather(0, d)
+        cast(1)
+        for d in range(TAPS):
+            gather(1, d)
+        for d in range(TAPS - 1):
+            weave(0, d, True)
+        for d in range(TAPS - 1):
+            multiply(0, d)
+        cast(2)
+        for d in range(TAPS):
+            gather(2, d)
+        cast(3)
+        weave(0, TAPS - 1, False)
+        for d in range(TAPS):
+            gather(3, d)
+            weave(1, d, False)
+        multiply(1, 0)
+        multiply(1, 1)
+        multiply(0, 2)
+        multiply(1, 2)
+
+        halves = U // BANK
+        blocks = BANK // P
+        turned = [psum.tile([P, BANK], F32, name=f"turned{h}") for h in range(halves)]
+        for d in range(TAPS - 1):
+            place(d)
+            for h in range(halves):
+                for b in range(blocks):
+                    col = h * BANK + b * P
+                    nc.tensor.matmul(
+                        turned[h][:, b * P : (b + 1) * P], placed[d][:, col : col + P], ident[:],
+                        start=(d == 0 and b == 0), stop=(d == TAPS - 2 and b == blocks - 1), is_transpose=True)
+        place(TAPS - 1)
+        for h in range(halves):
+            turned_sb = keep.tile([P, BANK], F32, name=f"turned_sb{h}")
+            nc.scalar.copy(out=turned_sb[:], in_=turned[h][:])
+            back = psum.tile([P, BANK], F32, name=f"back{h}")
+            for b in range(blocks):
+                nc.tensor.transpose(back[:, b * P : (b + 1) * P], turned_sb[:, b * P : (b + 1) * P], ident[:])
+            width = BANK // (h + 1)
+            for c0 in range(0, BANK, width):
+                total = keep.tile([P, width], F32, name=f"total{h}_{c0}")
+                cols = slice(h * BANK + c0, h * BANK + c0 + width)
+                nc.vector.tensor_tensor(out=total[:], in0=back[:, c0 : c0 + width], in1=placed[TAPS - 1][:, cols], op=ADD)
+                queue = nc.scalar if (h, c0) == (1, 0) else nc.sync
+                queue.dma_start(out=out[:, cols], in_=total[:])

@@ -24,7 +24,7 @@ LIST_COLS = V // 16
 
 CHUNKS = (
     ((1024, 0), (1024, 640)),
-    ((512, 0), (512, 0), (512, 0), (512, 320)),
+    ((1024, 0), (512, 512), (512, 320)),
     ((512, 0), (512, 0), (512, 0), (512, 0)),
     ((512, 0), (512, 0), (512, 0), (512, 256)),
 )
@@ -44,15 +44,9 @@ def tile_picked_spconv_none_e_kernel(tc, xT, w1_words, w1_scales, w2_words, w2_s
         offs_sb = keep.tile([P, TAPS * LIST_COLS], U16, name="offs_sb")
         to_sb = [keep.tile([P, LIST_COLS], U16, name=f"to{d}") for d in range(TAPS)]
         wq = [keep.tile([P, PASSES, 2 * N], U8, name=f"wq{d}", align_bytes=64) for d in range(TAPS)]
-        ws = [keep.tile([P, PASSES, N], U8, name=f"ws{d}", align_bytes=64) for d in range(TAPS)]
-        for d in range(TAPS):
-            nc.vector.memset(ws[d][:].bitcast(I32), 0)
-        for d in range(TAPS):
-            for q in range(4):
-                nc.gpsimd.dma_start(
-                    out=ws[d][32 * q : 32 * q + 4, :, :].bitcast(I32),
-                    in_=w_scales[d][:, 4 * q : 4 * q + 4, :].rearrange("g r c -> r g c").bitcast(I32),
-                )
+        ws = keep.tile([P, TAPS, PASSES, N], U8, name="ws", align_bytes=64)
+        ws_rows = ws[:].rearrange("p d g c -> p (d g c)").bitcast(I32)
+        nc.vector.memset(ws_rows, 0)
         ident = keep.tile([P, P], F32, name="ident")
         make_identity(nc, ident[:])
         placed = [keep.tile([P, U], F32, name=f"placed{d}") for d in range(TAPS)]
@@ -62,8 +56,14 @@ def tile_picked_spconv_none_e_kernel(tc, xT, w1_words, w1_scales, w2_words, w2_s
         small = [lambda: nc.sync.dma_start(offs_sb[:], offs)]
         for d in range(TAPS):
             small.append(lambda d=d: nc.sync.dma_start(
-                out=wq[d][:].bitcast(I32), in_=w_words[d].rearrange("g p c -> p g c").bitcast(I32)))
+                out=ws[0:16, d, :, :].bitcast(I32), in_=w_scales[d].rearrange("g r c -> r g c").bitcast(I32)))
+        small.append(lambda: nc.sync.dma_start(to_sb[0][:], to_lists[0]))
+        for q in range(1, 4):
+            small.append(lambda q=q: nc.sync.dma_start(out=ws_rows[32 * q : 32 * q + 4, :], in_=ws_rows[4 * q : 4 * q + 4, :]))
         for d in range(TAPS):
+            small.append(lambda d=d: nc.sync.dma_start(
+                out=wq[d][:].bitcast(I32), in_=w_words[d].rearrange("g p c -> p g c").bitcast(I32)))
+        for d in range(1, TAPS):
             small.append(lambda d=d: nc.sync.dma_start(to_sb[d][:], to_lists[d]))
 
         raw = {}
@@ -72,13 +72,12 @@ def tile_picked_spconv_none_e_kernel(tc, xT, w1_words, w1_scales, w2_words, w2_s
             for j, (width, vshare) in enumerate(CHUNKS[i]):
                 raw[i, j] = keep.tile([P, 2, width], F32, name=f"raw{i}_{j}", tag=f"raw{i}_{j}", align_bytes=64)
                 nc.sync.dma_start(out=raw[i, j][:], in_=x_rows[i // 2, i % 2][:, :, c0 : c0 + width])
-                if small and ((i, j) == (0, 0) or i >= 2):
-                    small.pop(0)()
+                small.pop(0)()
                 c0 = c0 + width
 
         pairs = [keep.tile([P, T, 2], BF16, name=f"pairs{i}", align_bytes=64) for i in range(4)]
         picked = {(g, d): keep.tile([P, 2, V], U32, name=f"picked{g}_{d}") for g in range(PASSES) for d in range(TAPS)}
-        acc = [psum.tile([P, V], F32, name=f"acc{d}") for d in range(TAPS)]
+        acc = [psum.tile([P, V], F32, name=f"acc{d}", tag=f"acc{d}") for d in range(TAPS)]
         quads = {}
 
         def cast(i):
@@ -100,7 +99,7 @@ def tile_picked_spconv_none_e_kernel(tc, xT, w1_words, w1_scales, w2_words, w2_s
             )
 
         def weave(g, d, on_vector):
-            tag = "raw3_3" if (g, d) == (0, TAPS - 1) else f"quads{g}_{d}"
+            tag = f"raw3_{len(CHUNKS[3]) - 1}" if (g, d) == (0, TAPS - 1) else f"quads{g}_{d}"
             quads[g, d] = keep.tile([P, 4 * V], BF16, name=f"quads{g}_{d}", tag=tag, align_bytes=64)
             if on_vector:
                 nc.vector.tensor_copy(
@@ -112,11 +111,12 @@ def tile_picked_spconv_none_e_kernel(tc, xT, w1_words, w1_scales, w2_words, w2_s
                     in_=picked[g, d][:].rearrange("p u v -> p v u"))
 
         def multiply(g, d):
-            codes = keep.tile([P, V], U32, name=f"codes{g}_{d}", align_bytes=64)
+            tag = "quads1_0" if (g, d) == (0, TAPS - 1) else f"codes{g}_{d}"
+            codes = keep.tile([P, V], U32, name=f"codes{g}_{d}", tag=tag, align_bytes=64)
             scales = keep.tile([P, V], U8, name=f"scales{g}_{d}", align_bytes=64)
             nc.vector.quantize_mx(out=codes[:].bitcast(FP8X4), scales=scales[:], in_=quads[g, d][:])
             nc.tensor.matmul_mx(
-                out=acc[d][:], lhsT=wq[d][:, g, :].bitcast(FP4X4), lhsT_scale=ws[d][:, g, :],
+                out=acc[d][:], lhsT=wq[d][:, g, :].bitcast(FP4X4), lhsT_scale=ws[:, d, g, :],
                 rhs=codes[:].bitcast(FP8X4), rhs_scale=scales[:], start=(g == 0), stop=(g == PASSES - 1))
 
         def place(d):
@@ -149,7 +149,8 @@ def tile_picked_spconv_none_e_kernel(tc, xT, w1_words, w1_scales, w2_words, w2_s
 
         halves = U // BANK
         blocks = BANK // P
-        turned = [psum.tile([P, BANK], F32, name=f"turned{h}") for h in range(halves)]
+        both = psum.tile([P, U], F32, name="both", tag=f"acc{TAPS - 1}")
+        turned = [both[:, h * BANK : (h + 1) * BANK] for h in range(halves)]
         for d in range(TAPS - 1):
             place(d)
             for h in range(halves):
@@ -161,7 +162,7 @@ def tile_picked_spconv_none_e_kernel(tc, xT, w1_words, w1_scales, w2_words, w2_s
         place(TAPS - 1)
         for h in range(halves):
             turned_sb = keep.tile([P, BANK], F32, name=f"turned_sb{h}")
-            nc.scalar.copy(out=turned_sb[:], in_=turned[h][:])
+            nc.scalar.copy(out=turned_sb[:], in_=turned[h])
             back = psum.tile([P, BANK], F32, name=f"back{h}")
             for b in range(blocks):
                 nc.tensor.transpose(back[:, b * P : (b + 1) * P], turned_sb[:, b * P : (b + 1) * P], ident[:])

@@ -23,8 +23,8 @@ BANK = 512
 LIST_COLS = V // 16
 
 CHUNKS = (
-    ((1024, 0), (1024, 640)),
-    ((1024, 0), (512, 512), (512, 320)),
+    ((1024, 1024), (512, 0), (512, 320)),
+    ((512, 0), (512, 0), (512, 0), (512, 320)),
     ((512, 0), (512, 0), (512, 0), (512, 0)),
     ((512, 0), (512, 0), (512, 0), (512, 256)),
 )
@@ -72,11 +72,12 @@ def tile_picked_spconv_none_e_kernel(tc, xT, w1_words, w1_scales, w2_words, w2_s
             for j, (width, vshare) in enumerate(CHUNKS[i]):
                 raw[i, j] = keep.tile([P, 2, width], F32, name=f"raw{i}_{j}", tag=f"raw{i}_{j}", align_bytes=64)
                 nc.sync.dma_start(out=raw[i, j][:], in_=x_rows[i // 2, i % 2][:, :, c0 : c0 + width])
-                small.pop(0)()
+                if small:
+                    small.pop(0)()
                 c0 = c0 + width
 
         pairs = [keep.tile([P, T, 2], BF16, name=f"pairs{i}", align_bytes=64) for i in range(4)]
-        picked = {(g, d): keep.tile([P, 2, V], U32, name=f"picked{g}_{d}") for g in range(PASSES) for d in range(TAPS)}
+        picked = [keep.tile([P, 2, TAPS * V], U32, name=f"picked{g}") for g in range(PASSES)]
         acc = [psum.tile([P, V], F32, name=f"acc{d}", tag=f"acc{d}") for d in range(TAPS)]
         quads = {}
 
@@ -91,11 +92,11 @@ def tile_picked_spconv_none_e_kernel(tc, xT, w1_words, w1_scales, w2_words, w2_s
                     nc.scalar.copy(out=pairs[i][:, c0 : c0 + s, :], in_=src[:, 0:s, :])
                 c0 = c0 + width
 
-        def gather(i, d):
+        def gather(i, d0, d1):
             window = pairs[i][:].rearrange("p t e -> p (t e)").bitcast(U32)
             nc.vector.tensor_copy(
-                out=picked[i // 2, d][:, i % 2, :],
-                in_=window.indirect(offs_sb[:, d * LIST_COLS : (d + 1) * LIST_COLS]),
+                out=picked[i // 2][:, i % 2, d0 * V : d1 * V],
+                in_=window.indirect(offs_sb[:, d0 * LIST_COLS : d1 * LIST_COLS]),
             )
 
         def weave(g, d, on_vector):
@@ -104,11 +105,11 @@ def tile_picked_spconv_none_e_kernel(tc, xT, w1_words, w1_scales, w2_words, w2_s
             if on_vector:
                 nc.vector.tensor_copy(
                     out=quads[g, d][:].bitcast(I32).rearrange("p (v u) -> p v u", u=2),
-                    in_=picked[g, d][:].bitcast(I32).rearrange("p u v -> p v u"))
+                    in_=picked[g][:, :, d * V : (d + 1) * V].bitcast(I32).rearrange("p u v -> p v u"))
             else:
                 nc.scalar.copy(
                     out=quads[g, d][:].bitcast(U32).rearrange("p (v u) -> p v u", u=2),
-                    in_=picked[g, d][:].rearrange("p u v -> p v u"))
+                    in_=picked[g][:, :, d * V : (d + 1) * V].rearrange("p u v -> p v u"))
 
         def multiply(g, d):
             tag = "quads1_0" if (g, d) == (0, TAPS - 1) else f"codes{g}_{d}"
@@ -125,22 +126,20 @@ def tile_picked_spconv_none_e_kernel(tc, xT, w1_words, w1_scales, w2_words, w2_s
             nc.vector.tensor_copy(out=placed[d][:].indirect(to_sb[d][:]), in_=y[:])
 
         cast(0)
-        for d in range(TAPS):
-            gather(0, d)
+        gather(0, 0, TAPS)
         cast(1)
-        for d in range(TAPS):
-            gather(1, d)
+        gather(1, 0, TAPS - 1)
+        gather(1, TAPS - 1, TAPS)
         for d in range(TAPS - 1):
             weave(0, d, True)
         for d in range(TAPS - 1):
             multiply(0, d)
         cast(2)
-        for d in range(TAPS):
-            gather(2, d)
+        gather(2, 0, TAPS)
         cast(3)
         weave(0, TAPS - 1, False)
         for d in range(TAPS):
-            gather(3, d)
+            gather(3, d, d + 1)
             weave(1, d, False)
         multiply(1, 0)
         multiply(1, 1)

@@ -19,23 +19,32 @@ ADD = mybir.AluOpType.add
 
 P = 128
 PASSES = 2
+TABLES = 2 * PASSES
 BANK = 512
 LIST_COLS = V // 16
+SCALE_ROWS = 16
+QUADRANT = 32
+PIECE = 256
 
+STEP = 512
 CHUNKS = (
-    ((1024, 1024), (512, 0), (512, 320)),
-    ((512, 0), (512, 0), (512, 0), (512, 320)),
-    ((512, 0), (512, 0), (512, 0), (512, 0)),
-    ((512, 0), (512, 0), (512, 0), (512, 256)),
+    ((3 * STEP, 2 * STEP), (STEP, STEP // 2)),
+    ((2 * STEP, 0), (STEP, STEP), (STEP, STEP // 2)),
+    ((STEP, 0), (STEP, 0), (STEP, 0), (STEP, 0)),
+    ((STEP, 0), (STEP, 0), (STEP, 0), (STEP, STEP // 2)),
 )
 
 
-def tile_picked_spconv_none_e_kernel(tc, xT, w1_words, w1_scales, w2_words, w2_scales, w3_words, w3_scales, offs, to1, to2, to3, out):
+def tile_picked_spconv_none_e_kernel(
+    tc, xT, w1_words, w1_scales, w2_words, w2_scales, w3_words, w3_scales, offs, to1, to2, to3, out
+):
     nc = tc.nc
     w_words = (w1_words, w2_words, w3_words)
     w_scales = (w1_scales, w2_scales, w3_scales)
     to_lists = (to1, to2, to3)
     x_rows = xT.rearrange("(g p u e) t -> g u p e t", g=PASSES, p=P, u=2, e=2)
+    last_tap = TAPS - 1
+    last_table = TABLES - 1
 
     with ExitStack() as ctx:
         keep = ctx.enter_context(tc.tile_pool(name="keep", bufs=1))
@@ -44,52 +53,56 @@ def tile_picked_spconv_none_e_kernel(tc, xT, w1_words, w1_scales, w2_words, w2_s
         offs_sb = keep.tile([P, TAPS * LIST_COLS], U16, name="offs_sb")
         to_sb = [keep.tile([P, LIST_COLS], U16, name=f"to{d}") for d in range(TAPS)]
         wq = [keep.tile([P, PASSES, 2 * N], U8, name=f"wq{d}", align_bytes=64) for d in range(TAPS)]
+
         ws = keep.tile([P, TAPS, PASSES, N], U8, name="ws", align_bytes=64)
         ws_rows = ws[:].rearrange("p d g c -> p (d g c)").bitcast(I32)
         nc.vector.memset(ws_rows, 0)
         ident = keep.tile([P, P], F32, name="ident")
         make_identity(nc, ident[:])
+
         placed = [keep.tile([P, U], F32, name=f"placed{d}") for d in range(TAPS)]
         for d in range(TAPS):
             nc.vector.memset(placed[d][:], 0.0)
 
-        small = [lambda: nc.sync.dma_start(offs_sb[:], offs)]
-        for d in range(TAPS):
-            small.append(lambda d=d: nc.sync.dma_start(
-                out=ws[0:16, d, :, :].bitcast(I32), in_=w_scales[d].rearrange("g r c -> r g c").bitcast(I32)))
-        small.append(lambda: nc.sync.dma_start(to_sb[0][:], to_lists[0]))
-        for q in range(1, 4):
-            small.append(lambda q=q: nc.sync.dma_start(out=ws_rows[32 * q : 32 * q + 4, :], in_=ws_rows[4 * q : 4 * q + 4, :]))
-        for d in range(TAPS):
-            small.append(lambda d=d: nc.sync.dma_start(
-                out=wq[d][:].bitcast(I32), in_=w_words[d].rearrange("g p c -> p g c").bitcast(I32)))
-        for d in range(1, TAPS):
-            small.append(lambda d=d: nc.sync.dma_start(to_sb[d][:], to_lists[d]))
-
         raw = {}
-        for i in range(4):
+        loads = 0
+        for i in range(TABLES):
             c0 = 0
-            for j, (width, vshare) in enumerate(CHUNKS[i]):
+            for j, (width, on_vector) in enumerate(CHUNKS[i]):
                 raw[i, j] = keep.tile([P, 2, width], F32, name=f"raw{i}_{j}", tag=f"raw{i}_{j}", align_bytes=64)
                 nc.sync.dma_start(out=raw[i, j][:], in_=x_rows[i // 2, i % 2][:, :, c0 : c0 + width])
-                if small:
-                    small.pop(0)()
+                if loads == 0:
+                    nc.sync.dma_start(offs_sb[:], offs)
+                elif loads <= TAPS:
+                    d = loads - 1
+                    nc.sync.dma_start(
+                        out=ws[0:SCALE_ROWS, d, :, :].bitcast(I32),
+                        in_=w_scales[d].rearrange("g r c -> r g c").bitcast(I32),
+                    )
+                if i == 2 and j >= 1:
+                    q = j
+                    nc.sync.dma_start(out=ws_rows[QUADRANT * q : QUADRANT * q + 4, :], in_=ws_rows[4 * q : 4 * q + 4, :])
+                loads = loads + 1
                 c0 = c0 + width
+        for d in range(TAPS):
+            nc.sync.dma_start(out=wq[d][:].bitcast(I32), in_=w_words[d].rearrange("g p c -> p g c").bitcast(I32))
+        for d in range(TAPS):
+            nc.sync.dma_start(to_sb[d][:], to_lists[d])
 
-        pairs = [keep.tile([P, T, 2], BF16, name=f"pairs{i}", align_bytes=64) for i in range(4)]
+        pairs = [keep.tile([P, T, 2], BF16, name=f"pairs{i}", align_bytes=64) for i in range(TABLES)]
         picked = [keep.tile([P, 2, TAPS * V], U32, name=f"picked{g}") for g in range(PASSES)]
         acc = [psum.tile([P, V], F32, name=f"acc{d}", tag=f"acc{d}") for d in range(TAPS)]
         quads = {}
 
-        def cast(i):
+        def round_table(i):
             c0 = 0
-            for j, (width, vshare) in enumerate(CHUNKS[i]):
-                s = width - vshare
+            for j, (width, on_vector) in enumerate(CHUNKS[i]):
+                on_scalar = width - on_vector
                 src = raw[i, j][:].rearrange("p e t -> p t e")
-                if vshare:
-                    nc.vector.tensor_copy(out=pairs[i][:, c0 + s : c0 + width, :], in_=src[:, s:width, :])
-                if s:
-                    nc.scalar.copy(out=pairs[i][:, c0 : c0 + s, :], in_=src[:, 0:s, :])
+                if on_vector:
+                    nc.vector.tensor_copy(out=pairs[i][:, c0 + on_scalar : c0 + width, :], in_=src[:, on_scalar:width, :])
+                if on_scalar:
+                    nc.scalar.copy(out=pairs[i][:, c0 : c0 + on_scalar, :], in_=src[:, 0:on_scalar, :])
                 c0 = c0 + width
 
         def gather(i, d0, d1):
@@ -99,76 +112,93 @@ def tile_picked_spconv_none_e_kernel(tc, xT, w1_words, w1_scales, w2_words, w2_s
                 in_=window.indirect(offs_sb[:, d0 * LIST_COLS : d1 * LIST_COLS]),
             )
 
-        def weave(g, d, on_vector):
-            tag = f"raw3_{len(CHUNKS[3]) - 1}" if (g, d) == (0, TAPS - 1) else f"quads{g}_{d}"
+        def weave(g, d, engine):
+            held = (g, d) == (0, last_tap)
+            tag = f"raw{last_table}_{len(CHUNKS[last_table]) - 1}" if held else f"quads{g}_{d}"
             quads[g, d] = keep.tile([P, 4 * V], BF16, name=f"quads{g}_{d}", tag=tag, align_bytes=64)
-            if on_vector:
+            words = picked[g][:, :, d * V : (d + 1) * V]
+            if engine == "vector":
                 nc.vector.tensor_copy(
                     out=quads[g, d][:].bitcast(I32).rearrange("p (v u) -> p v u", u=2),
-                    in_=picked[g][:, :, d * V : (d + 1) * V].bitcast(I32).rearrange("p u v -> p v u"))
+                    in_=words.bitcast(I32).rearrange("p u v -> p v u"),
+                )
             else:
                 nc.scalar.copy(
                     out=quads[g, d][:].bitcast(U32).rearrange("p (v u) -> p v u", u=2),
-                    in_=picked[g][:, :, d * V : (d + 1) * V].rearrange("p u v -> p v u"))
+                    in_=words.rearrange("p u v -> p v u"),
+                )
 
         def multiply(g, d):
-            tag = "quads1_0" if (g, d) == (0, TAPS - 1) else f"codes{g}_{d}"
+            held = (g, d) == (0, last_tap)
+            tag = f"quads{PASSES - 1}_0" if held else f"codes{g}_{d}"
             codes = keep.tile([P, V], U32, name=f"codes{g}_{d}", tag=tag, align_bytes=64)
             scales = keep.tile([P, V], U8, name=f"scales{g}_{d}", align_bytes=64)
             nc.vector.quantize_mx(out=codes[:].bitcast(FP8X4), scales=scales[:], in_=quads[g, d][:])
             nc.tensor.matmul_mx(
-                out=acc[d][:], lhsT=wq[d][:, g, :].bitcast(FP4X4), lhsT_scale=ws[:, d, g, :],
-                rhs=codes[:].bitcast(FP8X4), rhs_scale=scales[:], start=(g == 0), stop=(g == PASSES - 1))
+                out=acc[d][:],
+                lhsT=wq[d][:, g, :].bitcast(FP4X4),
+                lhsT_scale=ws[:, d, g, :],
+                rhs=codes[:].bitcast(FP8X4),
+                rhs_scale=scales[:],
+                start=(g == 0),
+                stop=(g == PASSES - 1),
+            )
 
         def place(d):
             y = keep.tile([P, V], F32, name=f"y{d}")
             nc.scalar.copy(out=y[:], in_=acc[d][:])
             nc.vector.tensor_copy(out=placed[d][:].indirect(to_sb[d][:]), in_=y[:])
 
-        cast(0)
+        round_table(0)
         gather(0, 0, TAPS)
-        cast(1)
-        gather(1, 0, TAPS - 1)
-        gather(1, TAPS - 1, TAPS)
-        for d in range(TAPS - 1):
-            weave(0, d, True)
-        for d in range(TAPS - 1):
+        round_table(1)
+        gather(1, 0, last_tap)
+        gather(1, last_tap, TAPS)
+        for d in range(last_tap):
+            weave(0, d, "vector")
+        for d in range(last_tap):
             multiply(0, d)
-        cast(2)
+
+        round_table(2)
         gather(2, 0, TAPS)
-        cast(3)
-        weave(0, TAPS - 1, False)
+        round_table(last_table)
+        weave(0, last_tap, "scalar")
         for d in range(TAPS):
-            gather(3, d, d + 1)
-            weave(1, d, False)
-        multiply(1, 0)
-        multiply(1, 1)
-        multiply(0, 2)
-        multiply(1, 2)
+            gather(last_table, d, d + 1)
+            weave(1, d, "scalar")
+        for d in range(last_tap):
+            multiply(1, d)
+        for g in range(PASSES):
+            multiply(g, last_tap)
 
         halves = U // BANK
         blocks = BANK // P
-        both = psum.tile([P, U], F32, name="both", tag=f"acc{TAPS - 1}")
+        both = psum.tile([P, U], F32, name="both", tag=f"acc{last_tap}")
         turned = [both[:, h * BANK : (h + 1) * BANK] for h in range(halves)]
-        for d in range(TAPS - 1):
+        for d in range(last_tap):
             place(d)
             for h in range(halves):
                 for b in range(blocks):
                     col = h * BANK + b * P
                     nc.tensor.matmul(
-                        turned[h][:, b * P : (b + 1) * P], placed[d][:, col : col + P], ident[:],
-                        start=(d == 0 and b == 0), stop=(d == TAPS - 2 and b == blocks - 1), is_transpose=True)
-        place(TAPS - 1)
+                        turned[h][:, b * P : (b + 1) * P],
+                        placed[d][:, col : col + P],
+                        ident[:],
+                        start=(d == 0 and b == 0),
+                        stop=(d == last_tap - 1 and b == blocks - 1),
+                        is_transpose=True,
+                    )
+        place(last_tap)
+
         for h in range(halves):
             turned_sb = keep.tile([P, BANK], F32, name=f"turned_sb{h}")
             nc.scalar.copy(out=turned_sb[:], in_=turned[h])
             back = psum.tile([P, BANK], F32, name=f"back{h}")
             for b in range(blocks):
                 nc.tensor.transpose(back[:, b * P : (b + 1) * P], turned_sb[:, b * P : (b + 1) * P], ident[:])
-            width = BANK // (h + 1)
-            for c0 in range(0, BANK, width):
-                total = keep.tile([P, width], F32, name=f"total{h}_{c0}")
-                cols = slice(h * BANK + c0, h * BANK + c0 + width)
-                nc.vector.tensor_tensor(out=total[:], in0=back[:, c0 : c0 + width], in1=placed[TAPS - 1][:, cols], op=ADD)
-                queue = nc.scalar if (h, c0) == (1, 0) else nc.sync
+            for c0 in range(0, BANK, PIECE):
+                total = keep.tile([P, PIECE], F32, name=f"total{h}_{c0}")
+                cols = slice(h * BANK + c0, h * BANK + c0 + PIECE)
+                nc.vector.tensor_tensor(out=total[:], in0=back[:, c0 : c0 + PIECE], in1=placed[last_tap][:, cols], op=ADD)
+                queue = nc.sync if c0 else nc.scalar
                 queue.dma_start(out=out[:, cols], in_=total[:])

from contextlib import ExitStack

import concourse.mybir as mybir
from concourse.masks import make_identity

K, T, V, N, U = 1024, 2048, 512, 128, 1024
TAPS = 3
FLOPS = 2 * K * N * TAPS * V

F32 = mybir.dt.float32
BF16 = mybir.dt.bfloat16
I32 = mybir.dt.int32
U32 = mybir.dt.uint32
U16 = mybir.dt.uint16
U8 = mybir.dt.uint8
FP8X4 = mybir.dt.float8_e4m3fn_x4
FP4X4 = mybir.dt.float4_e2m1fn_x4
ADD = mybir.AluOpType.add

P = 128
PASSES = 2
TABLES = 2 * PASSES
BANK = 512
LIST_COLS = V // 16
SCALE_ROWS = 16
QUADRANT = 32
PIECE = 256

STEP = 512
CHUNKS = (
    ((3 * STEP, 2 * STEP), (STEP, STEP // 2)),
    ((2 * STEP, 0), (STEP, STEP), (STEP, STEP // 2)),
    ((STEP, 0), (STEP, 0), (STEP, 0), (STEP, 0)),
    ((STEP, 0), (STEP, 0), (STEP, 0), (STEP, STEP // 2)),
)


def tile_picked_spconv_none_e_kernel(
    tc, xT, w1_words, w1_scales, w2_words, w2_scales, w3_words, w3_scales, offs, to1, to2, to3, out
):
    nc = tc.nc
    w_words = (w1_words, w2_words, w3_words)
    w_scales = (w1_scales, w2_scales, w3_scales)
    to_lists = (to1, to2, to3)
    x_rows = xT.rearrange("(g p u e) t -> g u p e t", g=PASSES, p=P, u=2, e=2)
    last_tap = TAPS - 1
    last_table = TABLES - 1

    with ExitStack() as ctx:
        keep = ctx.enter_context(tc.tile_pool(name="keep", bufs=1))
        psum = ctx.enter_context(tc.psum_pool(name="psum", bufs=1))

        offs_sb = keep.tile([P, TAPS * LIST_COLS], U16, name="offs_sb")
        to_sb = [keep.tile([P, LIST_COLS], U16, name=f"to{d}") for d in range(TAPS)]
        wq = [keep.tile([P, PASSES, 2 * N], U8, name=f"wq{d}", align_bytes=64) for d in range(TAPS)]

        ws = keep.tile([P, TAPS, PASSES, N], U8, name="ws", align_bytes=64)
        ws_rows = ws[:].rearrange("p d g c -> p (d g c)").bitcast(I32)
        nc.vector.memset(ws_rows, 0)
        ident = keep.tile([P, P], F32, name="ident")
        make_identity(nc, ident[:])

        placed = [keep.tile([P, U], F32, name=f"placed{d}") for d in range(TAPS)]
        for d in range(TAPS):
            nc.vector.memset(placed[d][:], 0.0)

        raw = {}
        loads = 0
        for i in range(TABLES):
            c0 = 0
            for j, (width, on_vector) in enumerate(CHUNKS[i]):
                raw[i, j] = keep.tile([P, 2, width], F32, name=f"raw{i}_{j}", tag=f"raw{i}_{j}", align_bytes=64)
                nc.sync.dma_start(out=raw[i, j][:], in_=x_rows[i // 2, i % 2][:, :, c0 : c0 + width])
                if loads == 0:
                    nc.sync.dma_start(offs_sb[:], offs)
                elif loads <= TAPS:
                    d = loads - 1
                    nc.sync.dma_start(
                        out=ws[0:SCALE_ROWS, d, :, :].bitcast(I32),
                        in_=w_scales[d].rearrange("g r c -> r g c").bitcast(I32),
                    )
                if i == 2 and j >= 1:
                    q = j
                    nc.sync.dma_start(out=ws_rows[QUADRANT * q : QUADRANT * q + 4, :], in_=ws_rows[4 * q : 4 * q + 4, :])
                loads = loads + 1
                c0 = c0 + width
        for d in range(TAPS):
            nc.sync.dma_start(out=wq[d][:].bitcast(I32), in_=w_words[d].rearrange("g p c -> p g c").bitcast(I32))
        for d in range(TAPS):
            nc.sync.dma_start(to_sb[d][:], to_lists[d])

        pairs = [keep.tile([P, T, 2], BF16, name=f"pairs{i}", align_bytes=64) for i in range(TABLES)]
        picked = [keep.tile([P, 2, TAPS * V], U32, name=f"picked{g}") for g in range(PASSES)]
        acc = [psum.tile([P, V], F32, name=f"acc{d}", tag=f"acc{d}") for d in range(TAPS)]
        quads = {}

        def round_table(i):
            c0 = 0
            for j, (width, on_vector) in enumerate(CHUNKS[i]):
                on_scalar = width - on_vector
                src = raw[i, j][:].rearrange("p e t -> p t e")
                if on_vector:
                    nc.vector.tensor_copy(out=pairs[i][:, c0 + on_scalar : c0 + width, :], in_=src[:, on_scalar:width, :])
                if on_scalar:
                    nc.scalar.copy(out=pairs[i][:, c0 : c0 + on_scalar, :], in_=src[:, 0:on_scalar, :])
                c0 = c0 + width

        def gather(i, d0, d1):
            window = pairs[i][:].rearrange("p t e -> p (t e)").bitcast(U32)
            nc.vector.tensor_copy(
                out=picked[i // 2][:, i % 2, d0 * V : d1 * V],
                in_=window.indirect(offs_sb[:, d0 * LIST_COLS : d1 * LIST_COLS]),
            )

        def weave(g, d, engine):
            held = (g, d) == (0, last_tap)
            tag = f"raw{last_table}_{len(CHUNKS[last_table]) - 1}" if held else f"quads{g}_{d}"
            quads[g, d] = keep.tile([P, 4 * V], BF16, name=f"quads{g}_{d}", tag=tag, align_bytes=64)
            words = picked[g][:, :, d * V : (d + 1) * V]
            if engine == "vector":
                nc.vector.tensor_copy(
                    out=quads[g, d][:].bitcast(I32).rearrange("p (v u) -> p v u", u=2),
                    in_=words.bitcast(I32).rearrange("p u v -> p v u"),
                )
            else:
                nc.scalar.copy(
                    out=quads[g, d][:].bitcast(U32).rearrange("p (v u) -> p v u", u=2),
                    in_=words.rearrange("p u v -> p v u"),
                )

        def multiply(g, d):
            held = (g, d) == (0, last_tap)
            tag = f"quads{PASSES - 1}_0" if held else f"codes{g}_{d}"
            codes = keep.tile([P, V], U32, name=f"codes{g}_{d}", tag=tag, align_bytes=64)
            scales = keep.tile([P, V], U8, name=f"scales{g}_{d}", align_bytes=64)
            nc.vector.quantize_mx(out=codes[:].bitcast(FP8X4), scales=scales[:], in_=quads[g, d][:])
            nc.tensor.matmul_mx(
                out=acc[d][:],
                lhsT=wq[d][:, g, :].bitcast(FP4X4),
                lhsT_scale=ws[:, d, g, :],
                rhs=codes[:].bitcast(FP8X4),
                rhs_scale=scales[:],
                start=(g == 0),
                stop=(g == PASSES - 1),
            )

        def place(d):
            y = keep.tile([P, V], F32, name=f"y{d}")
            nc.scalar.copy(out=y[:], in_=acc[d][:])
            nc.vector.tensor_copy(out=placed[d][:].indirect(to_sb[d][:]), in_=y[:])

        round_table(0)
        gather(0, 0, TAPS)
        round_table(1)
        gather(1, 0, last_tap)
        gather(1, last_tap, TAPS)
        for d in range(last_tap):
            weave(0, d, "vector")
        for d in range(last_tap):
            multiply(0, d)

        round_table(2)
        gather(2, 0, TAPS)
        round_table(last_table)
        weave(0, last_tap, "scalar")
        for d in range(TAPS):
            gather(last_table, d, d + 1)
            weave(1, d, "scalar")
        for d in range(last_tap):
            multiply(1, d)
        for g in range(PASSES):
            multiply(g, last_tap)

        halves = U // BANK
        blocks = BANK // P
        both = psum.tile([P, U], F32, name="both", tag=f"acc{last_tap}")
        turned = [both[:, h * BANK : (h + 1) * BANK] for h in range(halves)]
        for d in range(last_tap):
            place(d)
            for h in range(halves):
                for b in range(blocks):
                    col = h * BANK + b * P
                    nc.tensor.matmul(
                        turned[h][:, b * P : (b + 1) * P],
                        placed[d][:, col : col + P],
                        ident[:],
                        start=(d == 0 and b == 0),
                        stop=(d == last_tap - 1 and b == blocks - 1),
                        is_transpose=True,
                    )
        place(last_tap)

        for h in range(halves):
            turned_sb = keep.tile([P, BANK], F32, name=f"turned_sb{h}")
            nc.scalar.copy(out=turned_sb[:], in_=turned[h])
            back = psum.tile([P, BANK], F32, name=f"back{h}")
            for b in range(blocks):
                nc.tensor.transpose(back[:, b * P : (b + 1) * P], turned_sb[:, b * P : (b + 1) * P], ident[:])
            for c0 in range(0, BANK, PIECE):
                total = keep.tile([P, PIECE], F32, name=f"total{h}_{c0}")
                cols = slice(h * BANK + c0, h * BANK + c0 + PIECE)
                nc.vector.tensor_tensor(out=total[:], in0=back[:, c0 : c0 + PIECE], in1=placed[last_tap][:, cols], op=ADD)
                queue = nc.sync if c0 else nc.scalar
                queue.dma_start(out=out[:, cols], in_=total[:])
